import numpy as np
import ml_dtypes


def mxq(x, axis, fmt="e4m3"):
    dtype, down = {"e4m3": (ml_dtypes.float8_e4m3fn, 7), "e5m2": (ml_dtypes.float8_e5m2, 14)}[fmt]
    v = np.moveaxis(np.asarray(x, np.float32).astype(ml_dtypes.bfloat16).astype(np.float64), axis, -1)
    blocks = v.reshape(v.shape[:-1] + (-1, 32))
    amax = np.abs(blocks).max(-1, keepdims=True)
    byte = np.maximum(np.where(amax > 0, np.frexp(amax)[1] - 1 + 127, 0) - down, 1)
    scale = np.exp2(byte - 127.0)
    codes = (blocks / scale).astype(np.float32).astype(dtype).astype(np.float64)
    return np.moveaxis((codes * scale).reshape(v.shape), -1, axis)


WIDE = False


def mx_kscale(k):
    if not WIDE:
        return np.ones(k)
    levels = np.array([10, -10, 5, -5, 0])
    if k % 512:
        return np.exp2(np.random.permutation(np.resize(levels, k // 32))).repeat(32)
    a = np.empty((k // 512, 16))
    for p in range(k // 512):
        a[p, :8] = np.random.permutation(np.resize(levels, 8))
        for g in range(8):
            far = levels[np.abs(levels - a[p, g]) >= 10]
            a[p, g + 8] = far[np.random.randint(len(far))]
    return np.exp2(a.ravel()).repeat(32)


def f64(x):
    return np.asarray(x).astype(np.float64)


def striped(idx):
    return np.tile(idx.reshape(-1, 16).T, (8, 1)).astype(np.uint16)


def unstriped(offs):
    return offs[:16].T.reshape(-1).astype(np.int64)


E2M1 = np.array([0.0, 0.5, 1.0, 1.5, 2.0, 3.0, 4.0, 6.0, -0.0, -0.5, -1.0, -1.5, -2.0, -3.0, -4.0, -6.0])


def pack_weight(w, fmt):
    k, n = w.shape
    w = f64(np.asarray(w, np.float32).astype(ml_dtypes.bfloat16)).reshape(k // 32, 32, n)
    amax = np.abs(w).max(1)
    if fmt == "e4m3":
        byte = np.frexp(amax)[1] - 1 + 127 - 7
    else:
        mant, ex = np.frexp(amax / 6.0)
        byte = np.where(mant > 0.5, ex, ex - 1) + 127
    byte = np.clip(np.where(amax > 0, byte, 1), 1, 254)
    scaled = (w * np.exp2(127.0 - byte)[:, None, :]).reshape(k, n).astype(np.float32)
    by_word = np.ascontiguousarray(scaled.reshape(k // 512, 128, 4, n).transpose(0, 1, 3, 2))
    if fmt == "e4m3":
        words = by_word.astype(ml_dtypes.float8_e4m3fn).view(np.uint8)
    else:
        c = by_word.astype(ml_dtypes.float4_e2m1fn).view(np.uint8) & 0xF
        words = (c[..., 0::2] | (c[..., 1::2] << 4)).reshape(k // 512, 128, 2 * n)
    return np.ascontiguousarray(words), np.ascontiguousarray(byte.astype(np.uint8).reshape(k // 512, 16, n))


def unpack_weight(words, scales, fmt):
    g, _, n = scales.shape
    words = np.ascontiguousarray(words).reshape(g, 128, n, -1)
    if fmt == "e4m3":
        vals = words.view(ml_dtypes.float8_e4m3fn).astype(np.float64)
    else:
        nib = np.empty((g, 128, n, 4), np.uint8)
        nib[..., 0::2] = words & 0xF
        nib[..., 1::2] = words >> 4
        vals = E2M1[nib]
    vals = vals * np.repeat(np.exp2(scales.astype(np.float64) - 127.0), 8, axis=1)[..., None]
    return vals.transpose(0, 1, 3, 2).reshape(g * 512, n)


def gelu(v):
    return 0.5 * v * (1.0 + np.tanh(np.sqrt(2.0 / np.pi) * (v + 0.044715 * v**3)))


def striped8(idx):
    return np.concatenate([v.reshape(-1, 16).T for v in idx]).astype(np.uint16)


def unstriped8(offs):
    return np.stack([offs[16 * g:16 * g + 16].T.reshape(-1) for g in range(8)]).astype(np.int64)


def heads(h, wgt, idx8):
    r = np.arange(h.shape[0])
    return wgt[r // 4 % 128] * h[r[:, None], idx8[r % 512 // 64]]


def put_heads(h, wgs, idx8, t2):
    r = np.arange(h.shape[0])
    page = np.zeros((h.shape[0], t2))
    page[r[:, None], idx8[r % 512 // 64]] = wgs[r // 4 % 128] * h
    return page


K, H, N, T, S, T2, P = 1024, 1024, 384, 2048, 512, 1024, 512

def setup_inputs():
    n = np.random.standard_normal
    s = mx_kscale(K)[:, None]
    u = mx_kscale(H)[:, None]
    d = {}
    d["tab_words"], d["tab_scales"] = pack_weight(n((K, T)) * s, "e4m3")
    d["offs"] = striped(np.random.permutation(T)[:S])
    d["offs2"] = striped8(np.stack([np.random.permutation(T2)[:S] for _ in range(8)]))
    d["offs3"] = striped8(np.stack([np.random.permutation(T2)[:P] for _ in range(8)]))
    d["w1"] = (n((K, H)) / K ** 0.5 / s * u.T).astype(np.float32)
    d["b1"] = (0.5 * n(H) * u[:, 0]).astype(np.float32)
    d["w2_words"], d["w2_scales"] = pack_weight(0.8 * n((K, H)) / K ** 0.5 / s * u.T, "e4m3")
    d["w3_words"], d["w3_scales"] = pack_weight(n((K, H)) / K ** 0.5 / s * u.T, "e2m1")
    d["wgs"] = np.repeat(np.random.uniform(0.5, 2.0, (8, S)), 16, axis=0).astype(np.float32)
    d["wgt"] = np.repeat(np.random.uniform(0.5, 2.0, (8, P)), 16, axis=0).astype(np.float32)
    d["sand"] = (n((H, P)) * u).astype(np.float32)
    d["w4"] = (0.7 * n((H, N)) / H ** 0.5 / u).astype(np.float32)
    d["b4"] = (0.5 * n(N)).astype(np.float32)
    return d

def reference(tab_words, tab_scales, offs, offs2, offs3, w1, b1, w2_words, w2_scales,
              w3_words, w3_scales, wgs, wgt, sand, w4, b4):
    v = unpack_weight(tab_words, tab_scales, "e4m3")[:, unstriped(offs)]
    e1 = (mxq(f64(w1), 0, "e4m3").T @ v) + f64(b1)[:, None]
    e2 = np.abs(unpack_weight(w2_words, w2_scales, "e4m3").T @ v)
    e3 = unpack_weight(w3_words, w3_scales, "e2m1").T @ v
    h = np.maximum(np.maximum(e1, e2), e3)
    page = put_heads(h, f64(wgs), unstriped8(offs2), T2)
    x = heads(page, f64(wgt), unstriped8(offs3))
    zq = mxq(x + f64(sand), 0, "e4m3")
    y = mxq(f64(w4), 0, "e4m3").T @ zq
    return np.tanh(y + f64(b4)[:, None])

@@ -1,0 +1,313 @@
+from contextlib import ExitStack
+
+import concourse.mybir as mybir
+from concourse.masks import make_identity
+
+K, H, N, T, S, T2, PM = 1024, 1024, 384, 2048, 512, 1024, 512
+FLOPS = 2 * (3 * K * H * S + H * N * PM)
+
+F32 = mybir.dt.float32
+BF16 = mybir.dt.bfloat16
+I32 = mybir.dt.int32
+U32 = mybir.dt.uint32
+U16 = mybir.dt.uint16
+U8 = mybir.dt.uint8
+FP8X4 = mybir.dt.float8_e4m3fn_x4
+FP4X4 = mybir.dt.float4_e2m1fn_x4
+ALU = mybir.AluOpType
+ACT = mybir.ActivationFunctionType
+
+P = 128
+PACK = 4
+KP = P * PACK
+PASSES = K // KP
+HALVES = H // KP
+CHUNKS = S // P
+OUT_TILES = N // P
+
+
+def tile_list_nest_success_scores_kernel(
+    tc, tab_words, tab_scales, offs, offs2, offs3, w1, b1, w2_words, w2_scales,
+    w3_words, w3_scales, wgs, wgt, sand, w4, b4, out,
+):
+    nc = tc.nc
+    with ExitStack() as ctx:
+        lists = ctx.enter_context(tc.tile_pool(name="lists", bufs=1))
+        keep = ctx.enter_context(tc.tile_pool(name="keep", bufs=1))
+        ring = ctx.enter_context(tc.tile_pool(name="ring", bufs=2))
+        ring3 = ctx.enter_context(tc.tile_pool(name="ring3", bufs=3))
+        psum = ctx.enter_context(tc.psum_pool(name="psum", bufs=8))
+
+        def held(name, shape, dtype):
+            return keep.tile(shape, dtype, name=name, align_bytes=64)
+
+        pick = lists.tile([P, S // 16], U16, name="pick")
+        put = lists.tile([P, S // 16], U16, name="put")
+        fetch = lists.tile([P, PM // 16], U16, name="fetch")
+
+        tab_s = held("tab_s", [P, PASSES * T], U8)
+        w23_s = held("w23_s", [P, PASSES * H], U8)
+        pages = [held("page%d" % i, [P, T2], F32) for i in range(2)]
+        ident = held("ident", [P, P], F32)
+        nc.vector.memset(tab_s[:].bitcast(I32), 0)
+        for page in pages:
+            nc.vector.memset(page[:], 0.0)
+
+        tab_w = [held("tab_w%d" % a, [P, T], I32) for a in range(PASSES)]
+        w2_w = [held("w2_w%d" % b, [P, PASSES, KP], I32) for b in range(HALVES)]
+        w3_w = [held("w3_w%d" % b, [P, PASSES, 2 * KP], U8) for b in range(HALVES)]
+        w1_raw = {(b, a): held("w1_raw%d%d" % (b, a), [P, PACK, KP], F32) for b in range(HALVES) for a in range(PASSES)}
+        sand_sb = [held("sand%d" % b, [P, PACK, PM], F32) for b in range(HALVES)]
+        w4_raw = held("w4_raw", [P, HALVES, PACK, N], F32)
+        wgs_sb = held("wgs_sb", [P, S], F32)
+        wgt_sb = held("wgt_sb", [P, PM], F32)
+        b1_sb = held("b1_sb", [P, HALVES, PACK], F32)
+        b4_sb = held("b4_sb", [P, OUT_TILES], F32)
+
+        def load_scales(queue, plane, first_row, scales, quadrants):
+            for q in quadrants:
+                rows = plane[32 * q + first_row : 32 * q + first_row + 4, :].bitcast(I32)
+                queue.dma_start(
+                    rows.rearrange("r (a c) -> r a c", a=PASSES),
+                    scales[:, 4 * q : 4 * q + 4, :].bitcast(I32).rearrange("a r c -> r a c"),
+                )
+
+        def load_w23(b):
+            cols = slice(KP * b, KP * (b + 1))
+            nc.sync.dma_start(w2_w[b][:], w2_words[:, :, cols, :].rearrange("a p c i -> p a (c i)").bitcast(I32))
+            nc.sync.dma_start(
+                w3_w[b][:].bitcast(I32),
+                w3_words[:, :, 2 * KP * b : 2 * KP * (b + 1)].bitcast(I32).rearrange("a p c -> p a c"),
+            )
+
+        def load_w1(b):
+            for a in range(PASSES):
+                rows = w1[KP * a : KP * (a + 1), KP * b : KP * (b + 1)]
+                nc.sync.dma_start(w1_raw[b, a][:], rows.rearrange("(p j) c -> p j c", j=PACK))
+
+        def load_tab(a):
+            nc.sync.dma_start(tab_w[a][:], tab_words[a].rearrange("p t i -> p (t i)").bitcast(I32))
+
+        def load_sand(b):
+            nc.sync.dma_start(sand_sb[b][:], sand[KP * b : KP * (b + 1), :].rearrange("(p j) m -> p j m", j=PACK))
+
+        nc.sync.dma_start(pick[:], offs)
+        load_scales(nc.sync, w23_s, 0, w3_scales, range(4))
+        load_scales(nc.sync, w23_s, 4, w2_scales, range(2))
+        load_tab(0)
+        load_scales(nc.sync, tab_s, 0, tab_scales, range(4))
+        load_scales(nc.sync, w23_s, 4, w2_scales, range(2, 4))
+        load_w23(0)
+        load_tab(1)
+        load_w1(0)
+        nc.gpsimd.dma_start(b1_sb[:], b1.rearrange("(b p t) -> p b t", b=HALVES, t=PACK))
+        make_identity(nc, ident[:])
+        nc.sync.dma_start(put[:], offs2)
+        nc.sync.dma_start(wgs_sb[:], wgs)
+        nc.sync.dma_start(fetch[:], offs3)
+        nc.sync.dma_start(wgt_sb[:], wgt)
+        load_w23(1)
+        load_w1(1)
+        load_sand(0)
+        nc.sync.dma_start(w4_raw[:], w4.rearrange("(b p j) n -> p b j n", b=HALVES, j=PACK))
+        load_sand(1)
+        with nc.allow_non_contiguous_dma(reason="one bias value a partition"):
+            nc.sync.dma_start(b4_sb[:], b4.rearrange("(c p) -> p c", p=P))
+
+        v_w = [held("v_w%d" % a, [P, S], U32) for a in range(PASSES)]
+        v_s = [held("v_s%d" % a, [P, S], U8) for a in range(PASSES)]
+        for a in range(PASSES):
+            nc.vector.tensor_copy(v_s[a][:], tab_s[:, T * a : T * (a + 1)].indirect(pick[:]))
+            nc.vector.tensor_copy(v_w[a][:], tab_w[a][:].bitcast(U32).indirect(pick[:]))
+
+        m_t = {(b, jc): held("m_t%d%d" % (b, jc), [P, PACK, P], F32) for b in range(HALVES) for jc in range(CHUNKS)}
+
+        def bank():
+            return psum.tile([P, KP], F32, name="bank")
+
+        def multiply23(banks, b, jc, a):
+            js = slice(P * jc, P * (jc + 1))
+            cols = slice(H * a + KP * b, H * a + KP * (b + 1))
+            flags = dict(start=(a == 0), stop=(a == PASSES - 1))
+            nc.tensor.matmul_mx(
+                banks[0][:], lhsT=v_w[a][:, js].bitcast(FP8X4), lhsT_scale=v_s[a][:, js],
+                rhs=w2_w[b][:, a, :].bitcast(FP8X4), rhs_scale=w23_s[4:P, cols], **flags)
+            nc.tensor.matmul_mx(
+                banks[1][:], lhsT=v_w[a][:, js].bitcast(FP8X4), lhsT_scale=v_s[a][:, js],
+                rhs=w3_w[b][:, a, :].bitcast(FP4X4), rhs_scale=w23_s[:, cols], **flags)
+
+        def stronger23(banks, b, jc):
+            size = ring.tile([P, PACK, P], F32, name="size")
+            nc.scalar.activation(size[:], banks[0][:].rearrange("p (q t) -> p t q", t=PACK), ACT.Abs)
+            nc.vector.tensor_tensor(m_t[b, jc][:], banks[1][:].rearrange("p (q t) -> p t q", t=PACK), size[:], ALU.max)
+
+        def evidence23(b, jc):
+            banks = (bank(), bank())
+            for a in range(PASSES):
+                multiply23(banks, b, jc, a)
+            stronger23(banks, b, jc)
+
+        w1_bf = {key: held("w1_bf%d%d" % key, [P, PACK, P, PACK], BF16) for key in w1_raw}
+        w1_w = {key: held("w1_w%d%d" % key, [P, KP], U32) for key in w1_raw}
+        w1_s = {key: held("w1_s%d%d" % key, [P, KP], U8) for key in w1_raw}
+
+        def round_w1(copy, b, a, u):
+            src = w1_raw[b, a][:].rearrange("p j (m u e) -> p u m j e", u=2, e=2)[:, u]
+            dst = w1_bf[b, a][:, 2 * u : 2 * u + 2].rearrange("p e m j -> p m j e")
+            copy(dst, src)
+
+        def quantize_w1(b, a, ts):
+            cols = slice(P * ts.start, P * ts.stop)
+            nc.vector.quantize_mx(
+                w1_w[b, a][:, cols].bitcast(FP8X4), w1_s[b, a][:, cols],
+                w1_bf[b, a][:, ts].rearrange("p t m j -> p (t m j)"))
+
+        h_tiles = {}
+
+        def strongest(s):
+            b, t = divmod(s, PACK)
+            turned = bank()
+            for jc in range(CHUNKS):
+                nc.tensor.transpose(turned[:, P * jc : P * (jc + 1)], m_t[b, jc][:, t, :], ident[:])
+            m23 = ring3.tile([P, S], F32, name="m23")
+            nc.scalar.copy(m23[:], turned[:])
+            e1 = bank()
+            cols = slice(P * t, P * (t + 1))
+            for a in range(PASSES):
+                nc.tensor.matmul_mx(
+                    e1[:], lhsT=w1_w[b, a][:, cols].bitcast(FP8X4), lhsT_scale=w1_s[b, a][:, cols],
+                    rhs=v_w[a][:].bitcast(FP8X4), rhs_scale=v_s[a][:],
+                    start=(a == 0), stop=(a == PASSES - 1))
+            h = ring3.tile([P, S], F32, name="h")
+            nc.vector.scalar_tensor_tensor(h[:], e1[:], b1_sb[:, b, t : t + 1], m23[:], ALU.add, ALU.max)
+            h_tiles[s] = h
+
+        x_sb = [held("x%d" % b, [P, PACK, PM], F32) for b in range(HALVES)]
+        z_bf = [held("z_bf%d" % b, [P, PM, PACK], BF16) for b in range(HALVES)]
+        z_w = [held("z_w%d" % b, [P, PM], U32) for b in range(HALVES)]
+        z_s = [held("z_s%d" % b, [P, PM], U8) for b in range(HALVES)]
+        w4_bf = held("w4_bf", [P, HALVES, N, PACK], BF16)
+        w4_w = held("w4_w", [P, HALVES * N], U32)
+        w4_s = held("w4_s", [P, HALVES * N], U8)
+
+        def enter(s):
+            nc.vector.tensor_tensor(pages[s % 2][:].indirect(put[:]), h_tiles[s][:], wgs_sb[:], ALU.mult)
+
+        def read(s):
+            b, t = divmod(s, PACK)
+            nc.vector.tensor_tensor(x_sb[b][:, t, :], pages[s % 2][:].indirect(fetch[:]), wgt_sb[:], ALU.mult)
+
+        def add_sand(b, ms):
+            rows = lambda tile: tile[:, :, ms].rearrange("p t (c i) -> p c t i", i=4)
+            nc.vector.tensor_tensor(
+                z_bf[b][:, ms, :].rearrange("p (c i) t -> p c t i", i=4), rows(x_sb[b]), rows(sand_sb[b]), ALU.add)
+
+        def quantize_z(b, ms):
+            nc.vector.quantize_mx(
+                z_w[b][:, ms].bitcast(FP8X4), z_s[b][:, ms], z_bf[b][:, ms, :].rearrange("p m t -> p (m t)"))
+
+        def round_w4(b):
+            nc.scalar.copy(
+                w4_bf[:, b].rearrange("p (c i) j -> p c j i", i=4),
+                w4_raw[:, b].rearrange("p j (c i) -> p c j i", i=4))
+
+        def quantize_w4(lo, hi):
+            flat = w4_bf[:].rearrange("p b n j -> p (b n j)")
+            nc.vector.quantize_mx(w4_w[:, lo:hi].bitcast(FP8X4), w4_s[:, lo:hi], flat[:, PACK * lo : PACK * hi])
+
+        half = PM // 2
+        sums = {}
+        pairs = [held("pairs%d" % u, [P, CHUNKS, P, 2], BF16) for u in range(2)]
+
+        def turn_and_add(t):
+            u, e = divmod(t, 2)
+            for c in range(CHUNKS):
+                if (u, c // 2) not in sums:
+                    sums[u, c // 2] = bank()
+                block = sums[u, c // 2][:, P * (2 * (c % 2) + e) : P * (2 * (c % 2) + e + 1)]
+                ms = slice(P * c, P * (c + 1))
+                nc.tensor.matmul(block, lhsT=sand_sb[0][:, t, ms], rhs=ident[:], is_transpose=True, start=True, stop=False)
+                nc.tensor.matmul(block, lhsT=x_sb[0][:, t, ms], rhs=ident[:], is_transpose=True, start=False, stop=True)
+            if e == 1:
+                for mh in range(2):
+                    nc.scalar.copy(
+                        pairs[u][:, 2 * mh : 2 * mh + 2],
+                        sums[u, mh][:].rearrange("m (c e p) -> m c p e", c=2, e=2))
+
+        def turn_back():
+            for mh in range(2):
+                back = bank()
+                for u in range(2):
+                    for c in range(2):
+                        words = pairs[u][:, 2 * mh + c].rearrange("m p e -> m (p e)").bitcast(F32)
+                        nc.tensor.transpose(back[:, half * u + P * c : half * u + P * (c + 1)], words, ident[:])
+                z_words = z_bf[0][:, half * mh : half * (mh + 1), :].rearrange("p m t -> p (m t)").bitcast(F32)
+                nc.scalar.copy(z_words.rearrange("p (m u) -> p m u", u=2), back[:].rearrange("p (u m) -> p m u", u=2))
+
+        first = [(bank(), bank()) for jc in range(CHUNKS)]
+        for jc in range(CHUNKS):
+            multiply23(first[jc], 0, jc, 0)
+        for jc in range(CHUNKS):
+            multiply23(first[jc], 0, jc, 1)
+            stronger23(first[jc], 0, jc)
+        round_w1(nc.scalar.copy, 0, 0, 0)
+        quantize_w1(0, 0, slice(0, 2))
+        round_w1(nc.vector.tensor_copy, 0, 1, 0)
+        quantize_w1(0, 1, slice(0, 2))
+        strongest(0)
+        strongest(1)
+        slices = HALVES * PACK
+        for s in range(slices):
+            enter(s)
+            if s == 0:
+                for a in range(PASSES):
+                    round_w1(nc.scalar.copy, 0, a, 1)
+                    quantize_w1(0, a, slice(2, 4))
+                for jc in range(CHUNKS):
+                    evidence23(1, jc)
+                for a in range(PASSES):
+                    for u in range(2):
+                        round_w1(nc.scalar.copy, 1, a, u)
+            if s == 1:
+                for a in range(PASSES):
+                    quantize_w1(1, a, slice(0, 4))
+            if s == 4:
+                for b in range(HALVES):
+                    round_w4(b)
+            if s + 2 < slices:
+                strongest(s + 2)
+            if s == 6:
+                quantize_z(0, slice(0, half))
+            if s == 7:
+                quantize_z(0, slice(half, PM))
+            read(s)
+            if s < PACK:
+                turn_and_add(s)
+            if s == PACK - 1:
+                turn_back()
+
+        res = held("res", [P, OUT_TILES, PM], F32)
+        y = {(mh, c): bank() for mh in range(2) for c in range(OUT_TILES)}
+
+        def score(b, mh, c):
+            ms = slice(half * mh, half * (mh + 1))
+            cols = slice(N * b + P * c, N * b + P * (c + 1))
+            nc.tensor.matmul_mx(
+                y[mh, c][:, 0:half], lhsT=w4_w[:, cols].bitcast(FP8X4), lhsT_scale=w4_s[:, cols],
+                rhs=z_w[b][:, ms].bitcast(FP8X4), rhs_scale=z_s[b][:, ms],
+                start=(b == 0), stop=(b == HALVES - 1))
+
+        quantize_w4(0, 512)
+        add_sand(1, slice(0, half))
+        quantize_w4(512, 768)
+        for mh, c in y:
+            score(0, mh, c)
+        for mh in range(2):
+            ms = slice(half * mh, half * (mh + 1))
+            if mh == 1:
+                add_sand(1, ms)
+            quantize_z(1, ms)
+            for c in range(OUT_TILES):
+                score(1, mh, c)
+                nc.scalar.activation(res[:, c, ms], y[mh, c][:, 0:half], ACT.Tanh, bias=b4_sb[:, c : c + 1])
+                nc.sync.dma_start(out[P * c : P * (c + 1), ms], res[:, c, ms])

@@ -36,7 +36,7 @@ def tile_list_nest_success_scores_kernel(
         keep = ctx.enter_context(tc.tile_pool(name="keep", bufs=1))
         ring = ctx.enter_context(tc.tile_pool(name="ring", bufs=2))
         ring3 = ctx.enter_context(tc.tile_pool(name="ring3", bufs=3))
-        psum = ctx.enter_context(tc.psum_pool(name="psum", bufs=8))
+        psum = ctx.enter_context(tc.psum_pool(name="psum", bufs=1))
 
         def held(name, shape, dtype):
             return keep.tile(shape, dtype, name=name, align_bytes=64)
@@ -99,6 +99,7 @@ def tile_list_nest_success_scores_kernel(
         load_scales(nc.sync, w23_s, 4, w2_scales, range(2, 4))
         load_w23(0)
         load_tab(1)
+        load_w23(1)
         load_w1(0)
         nc.gpsimd.dma_start(b1_sb[:], b1.rearrange("(b p t) -> p b t", b=HALVES, t=PACK))
         make_identity(nc, ident[:])
@@ -106,7 +107,6 @@ def tile_list_nest_success_scores_kernel(
         nc.sync.dma_start(wgs_sb[:], wgs)
         nc.sync.dma_start(fetch[:], offs3)
         nc.sync.dma_start(wgt_sb[:], wgt)
-        load_w23(1)
         load_w1(1)
         load_sand(0)
         nc.sync.dma_start(w4_raw[:], w4.rearrange("(b p j) n -> p b j n", b=HALVES, j=PACK))
@@ -120,10 +120,10 @@ def tile_list_nest_success_scores_kernel(
             nc.vector.tensor_copy(v_s[a][:], tab_s[:, T * a : T * (a + 1)].indirect(pick[:]))
             nc.vector.tensor_copy(v_w[a][:], tab_w[a][:].bitcast(U32).indirect(pick[:]))
 
-        m_t = {(b, jc): held("m_t%d%d" % (b, jc), [P, PACK, P], F32) for b in range(HALVES) for jc in range(CHUNKS)}
+        m_t = {(b, jc): held("m_t%d%d" % (b, jc), [P, 2, P, 2], F32) for b in range(HALVES) for jc in range(CHUNKS)}
 
-        def bank():
-            return psum.tile([P, KP], F32, name="bank")
+        def bank(i):
+            return psum.tile([P, KP], F32, name="bank%d" % i)
 
         def multiply23(banks, b, jc, a):
             js = slice(P * jc, P * (jc + 1))
@@ -137,12 +137,13 @@ def tile_list_nest_success_scores_kernel(
                 rhs=w3_w[b][:, a, :].bitcast(FP4X4), rhs_scale=w23_s[:, cols], **flags)
 
         def stronger23(banks, b, jc):
-            size = ring.tile([P, PACK, P], F32, name="size")
-            nc.scalar.activation(size[:], banks[0][:].rearrange("p (q t) -> p t q", t=PACK), ACT.Abs)
-            nc.vector.tensor_tensor(m_t[b, jc][:], banks[1][:].rearrange("p (q t) -> p t q", t=PACK), size[:], ALU.max)
+            size = ring.tile([P, 2, P, 2], F32, name="size")
+            dealt = [acc[:].rearrange("p (q u e) -> p u q e", u=2, e=2) for acc in banks]
+            nc.scalar.activation(size[:], dealt[0], ACT.Abs)
+            nc.vector.tensor_tensor(m_t[b, jc][:], dealt[1], size[:], ALU.max)
 
         def evidence23(b, jc):
-            banks = (bank(), bank())
+            banks = (bank(4 + 2 * (jc % 2)), bank(5 + 2 * (jc % 2)))
             for a in range(PASSES):
                 multiply23(banks, b, jc, a)
             stronger23(banks, b, jc)
@@ -164,26 +165,48 @@ def tile_list_nest_success_scores_kernel(
 
         h_tiles = {}
 
+        def turn(dst, src, start, stop):
+            nc.tensor.matmul(dst, lhsT=src, rhs=ident[:], is_transpose=True, start=start, stop=stop)
+
         def strongest(s):
             b, t = divmod(s, PACK)
-            turned = bank()
+            blocks = [slice(P * jc, P * (jc + 1)) for jc in range(CHUNKS)]
+            m_rows = [m_t[b, jc][:, t // 2, :, t % 2] for jc in range(CHUNKS)]
+            turned = bank(2 * (s % 2))
             for jc in range(CHUNKS):
-                nc.tensor.transpose(turned[:, P * jc : P * (jc + 1)], m_t[b, jc][:, t, :], ident[:])
-            m23 = ring3.tile([P, S], F32, name="m23")
-            nc.scalar.copy(m23[:], turned[:])
-            e1 = bank()
+                turn(turned[:, blocks[jc]], m_rows[jc], True, True)
+            e1 = bank(2 * (s % 2) + 1)
             cols = slice(P * t, P * (t + 1))
             for a in range(PASSES):
                 nc.tensor.matmul_mx(
                     e1[:], lhsT=w1_w[b, a][:, cols].bitcast(FP8X4), lhsT_scale=w1_s[b, a][:, cols],
                     rhs=v_w[a][:].bitcast(FP8X4), rhs_scale=v_s[a][:],
                     start=(a == 0), stop=(a == PASSES - 1))
+            m23 = ring.tile([P, S], F32, name="m23")
             h = ring3.tile([P, S], F32, name="h")
-            nc.vector.scalar_tensor_tensor(h[:], e1[:], b1_sb[:, b, t : t + 1], m23[:], ALU.add, ALU.max)
+            bias = b1_sb[:, b, t : t + 1]
             h_tiles[s] = h
+            if s < 2:
+                nc.scalar.copy(m23[:], turned[:])
+                nc.vector.scalar_tensor_tensor(h[:], e1[:], bias, m23[:], ALU.add, ALU.max)
+                return
+            nc.scalar.activation(m23[:], turned[:], ACT.Copy, scale=-1.0)
+            first = ring.tile([P, S], F32, name="first")
+            nc.scalar.activation(first[:], e1[:], ACT.Identity, bias=bias)
+            lead = bank(2 * (s % 2))
+            for jc in range(CHUNKS):
+                turn(lead[:, blocks[jc]], m23[:, blocks[jc]], True, False)
+                turn(lead[:, blocks[jc]], first[:, blocks[jc]], False, True)
+            excess = ring.tile([P, S], F32, name="excess")
+            nc.scalar.activation(excess[:], lead[:], ACT.Relu)
+            total = bank(2 * (s % 2) + 1)
+            for jc in range(CHUNKS):
+                turn(total[:, blocks[jc]], m_rows[jc], True, False)
+                turn(total[:, blocks[jc]], excess[:, blocks[jc]], False, True)
+            nc.scalar.copy(h[:], total[:])
 
         x_sb = [held("x%d" % b, [P, PACK, PM], F32) for b in range(HALVES)]
-        z_bf = [held("z_bf%d" % b, [P, PM, PACK], BF16) for b in range(HALVES)]
+        z_bf = held("z_bf", [P, PM, PACK], BF16)
         z_w = [held("z_w%d" % b, [P, PM], U32) for b in range(HALVES)]
         z_s = [held("z_s%d" % b, [P, PM], U8) for b in range(HALVES)]
         w4_bf = held("w4_bf", [P, HALVES, N, PACK], BF16)
@@ -200,11 +223,11 @@ def tile_list_nest_success_scores_kernel(
         def add_sand(b, ms):
             rows = lambda tile: tile[:, :, ms].rearrange("p t (c i) -> p c t i", i=4)
             nc.vector.tensor_tensor(
-                z_bf[b][:, ms, :].rearrange("p (c i) t -> p c t i", i=4), rows(x_sb[b]), rows(sand_sb[b]), ALU.add)
+                z_bf[:, ms, :].rearrange("p (c i) t -> p c t i", i=4), rows(x_sb[b]), rows(sand_sb[b]), ALU.add)
 
         def quantize_z(b, ms):
             nc.vector.quantize_mx(
-                z_w[b][:, ms].bitcast(FP8X4), z_s[b][:, ms], z_bf[b][:, ms, :].rearrange("p m t -> p (m t)"))
+                z_w[b][:, ms].bitcast(FP8X4), z_s[b][:, ms], z_bf[:, ms, :].rearrange("p m t -> p (m t)"))
 
         def round_w4(b):
             nc.scalar.copy(
@@ -223,7 +246,7 @@ def tile_list_nest_success_scores_kernel(
             u, e = divmod(t, 2)
             for c in range(CHUNKS):
                 if (u, c // 2) not in sums:
-                    sums[u, c // 2] = bank()
+                    sums[u, c // 2] = bank((2 + 2 * u + c // 2) % 4)
                 block = sums[u, c // 2][:, P * (2 * (c % 2) + e) : P * (2 * (c % 2) + e + 1)]
                 ms = slice(P * c, P * (c + 1))
                 nc.tensor.matmul(block, lhsT=sand_sb[0][:, t, ms], rhs=ident[:], is_transpose=True, start=True, stop=False)
@@ -236,25 +259,27 @@ def tile_list_nest_success_scores_kernel(
 
         def turn_back():
             for mh in range(2):
-                back = bank()
+                back = bank(4 + mh)
                 for u in range(2):
                     for c in range(2):
                         words = pairs[u][:, 2 * mh + c].rearrange("m p e -> m (p e)").bitcast(F32)
                         nc.tensor.transpose(back[:, half * u + P * c : half * u + P * (c + 1)], words, ident[:])
-                z_words = z_bf[0][:, half * mh : half * (mh + 1), :].rearrange("p m t -> p (m t)").bitcast(F32)
+                z_words = z_bf[:, half * mh : half * (mh + 1), :].rearrange("p m t -> p (m t)").bitcast(F32)
                 nc.scalar.copy(z_words.rearrange("p (m u) -> p m u", u=2), back[:].rearrange("p (u m) -> p m u", u=2))
 
-        first = [(bank(), bank()) for jc in range(CHUNKS)]
+        opening = [(bank(2 * jc), bank(2 * jc + 1)) for jc in range(CHUNKS)]
         for jc in range(CHUNKS):
-            multiply23(first[jc], 0, jc, 0)
+            multiply23(opening[jc], 0, jc, 0)
         for jc in range(CHUNKS):
-            multiply23(first[jc], 0, jc, 1)
-            stronger23(first[jc], 0, jc)
+            multiply23(opening[jc], 0, jc, 1)
+            stronger23(opening[jc], 0, jc)
         round_w1(nc.scalar.copy, 0, 0, 0)
         quantize_w1(0, 0, slice(0, 2))
         round_w1(nc.vector.tensor_copy, 0, 1, 0)
         quantize_w1(0, 1, slice(0, 2))
         strongest(0)
+        for jc in range(CHUNKS):
+            evidence23(1, jc)
         strongest(1)
         slices = HALVES * PACK
         for s in range(slices):
@@ -263,12 +288,7 @@ def tile_list_nest_success_scores_kernel(
                 for a in range(PASSES):
                     round_w1(nc.scalar.copy, 0, a, 1)
                     quantize_w1(0, a, slice(2, 4))
-                for jc in range(CHUNKS):
-                    evidence23(1, jc)
-                for a in range(PASSES):
-                    for u in range(2):
-                        round_w1(nc.scalar.copy, 1, a, u)
-            if s == 1:
+            if s == 2:
                 for a in range(PASSES):
                     quantize_w1(1, a, slice(0, 4))
             if s == 4:
@@ -276,18 +296,18 @@ def tile_list_nest_success_scores_kernel(
                     round_w4(b)
             if s + 2 < slices:
                 strongest(s + 2)
-            if s == 6:
-                quantize_z(0, slice(0, half))
-            if s == 7:
-                quantize_z(0, slice(half, PM))
+            if s == 1:
+                for a in range(PASSES):
+                    for u in range(2):
+                        round_w1(nc.scalar.copy, 1, a, u)
             read(s)
-            if s < PACK:
-                turn_and_add(s)
-            if s == PACK - 1:
-                turn_back()
+        for t in range(PACK):
+            turn_and_add(t)
+        turn_back()
+        quantize_z(0, slice(0, PM))
 
         res = held("res", [P, OUT_TILES, PM], F32)
-        y = {(mh, c): bank() for mh in range(2) for c in range(OUT_TILES)}
+        y = {(mh, c): bank((6 + OUT_TILES * mh + c) % 8) for mh in range(2) for c in range(OUT_TILES)}
 
         def score(b, mh, c):
             ms = slice(half * mh, half * (mh + 1))

@@ -47,7 +47,7 @@ def tile_list_nest_success_scores_kernel(
 
         tab_s = held("tab_s", [P, PASSES * T], U8)
         w23_s = held("w23_s", [P, PASSES * H], U8)
-        pages = [held("page%d" % i, [P, T2], F32) for i in range(2)]
+        pages = [held("page%d" % i, [P, T2], F32) for i in range(3)]
         ident = held("ident", [P, P], F32)
         nc.vector.memset(tab_s[:].bitcast(I32), 0)
         for page in pages:
@@ -96,9 +96,9 @@ def tile_list_nest_success_scores_kernel(
         load_scales(nc.sync, w23_s, 4, w2_scales, range(2))
         load_tab(0)
         load_scales(nc.sync, tab_s, 0, tab_scales, range(4))
-        load_scales(nc.sync, w23_s, 4, w2_scales, range(2, 4))
         load_w23(0)
         load_tab(1)
+        load_scales(nc.sync, w23_s, 4, w2_scales, range(2, 4))
         load_w23(1)
         load_w1(0)
         nc.gpsimd.dma_start(b1_sb[:], b1.rearrange("(b p t) -> p b t", b=HALVES, t=PACK))
@@ -125,16 +125,18 @@ def tile_list_nest_success_scores_kernel(
         def bank(i):
             return psum.tile([P, KP], F32, name="bank%d" % i)
 
-        def multiply23(banks, b, jc, a):
+        def multiply(acc, words, plane, b, jc, a):
             js = slice(P * jc, P * (jc + 1))
-            cols = slice(H * a + KP * b, H * a + KP * (b + 1))
-            flags = dict(start=(a == 0), stop=(a == PASSES - 1))
             nc.tensor.matmul_mx(
-                banks[0][:], lhsT=v_w[a][:, js].bitcast(FP8X4), lhsT_scale=v_s[a][:, js],
-                rhs=w2_w[b][:, a, :].bitcast(FP8X4), rhs_scale=w23_s[4:P, cols], **flags)
-            nc.tensor.matmul_mx(
-                banks[1][:], lhsT=v_w[a][:, js].bitcast(FP8X4), lhsT_scale=v_s[a][:, js],
-                rhs=w3_w[b][:, a, :].bitcast(FP4X4), rhs_scale=w23_s[:, cols], **flags)
+                acc[:], lhsT=v_w[a][:, js].bitcast(FP8X4), lhsT_scale=v_s[a][:, js],
+                rhs=words, rhs_scale=plane[:, H * a + KP * b : H * a + KP * (b + 1)],
+                start=(a == 0), stop=(a == PASSES - 1))
+
+        def multiply2(acc, b, jc, a):
+            multiply(acc, w2_w[b][:, a, :].bitcast(FP8X4), w23_s[4:P, :], b, jc, a)
+
+        def multiply3(acc, b, jc, a):
+            multiply(acc, w3_w[b][:, a, :].bitcast(FP4X4), w23_s[:, :], b, jc, a)
 
         def stronger23(banks, b, jc):
             size = ring.tile([P, 2, P, 2], F32, name="size")
@@ -145,7 +147,8 @@ def tile_list_nest_success_scores_kernel(
         def evidence23(b, jc):
             banks = (bank(4 + 2 * (jc % 2)), bank(5 + 2 * (jc % 2)))
             for a in range(PASSES):
-                multiply23(banks, b, jc, a)
+                multiply2(banks[0], b, jc, a)
+                multiply3(banks[1], b, jc, a)
             stronger23(banks, b, jc)
 
         w1_bf = {key: held("w1_bf%d%d" % key, [P, PACK, P, PACK], BF16) for key in w1_raw}
@@ -197,16 +200,20 @@ def tile_list_nest_success_scores_kernel(
             for jc in range(CHUNKS):
                 turn(lead[:, blocks[jc]], m23[:, blocks[jc]], True, False)
                 turn(lead[:, blocks[jc]], first[:, blocks[jc]], False, True)
-            excess = ring.tile([P, S], F32, name="excess")
-            nc.scalar.activation(excess[:], lead[:], ACT.Relu)
+            excess = x_rows[s - 2]
+            nc.scalar.activation(excess, lead[:], ACT.Relu)
             total = bank(2 * (s % 2) + 1)
             for jc in range(CHUNKS):
                 turn(total[:, blocks[jc]], m_rows[jc], True, False)
                 turn(total[:, blocks[jc]], excess[:, blocks[jc]], False, True)
             nc.scalar.copy(h[:], total[:])
 
-        x_sb = [held("x%d" % b, [P, PACK, PM], F32) for b in range(HALVES)]
-        z_bf = held("z_bf", [P, PM, PACK], BF16)
+        half = PM // 2
+        x_two = [held("x%d" % i, [P, 2, PM], F32) for i in range(2 * HALVES)]
+        x_rows = [x_two[s // 2][:, s % 2, :] for s in range(HALVES * PACK)]
+        z_last = [held("z_last%d" % mh, [P, PM], F32) for mh in range(2)]
+        z_flat = [x_rows[-2:], [tile[:] for tile in z_last]]
+        z_two = [held("z_two%d" % mh, [P, 2, half], F32) for mh in range(2)]
         z_w = [held("z_w%d" % b, [P, PM], U32) for b in range(HALVES)]
         z_s = [held("z_s%d" % b, [P, PM], U8) for b in range(HALVES)]
         w4_bf = held("w4_bf", [P, HALVES, N, PACK], BF16)
@@ -214,20 +221,23 @@ def tile_list_nest_success_scores_kernel(
         w4_s = held("w4_s", [P, HALVES * N], U8)
 
         def enter(s):
-            nc.vector.tensor_tensor(pages[s % 2][:].indirect(put[:]), h_tiles[s][:], wgs_sb[:], ALU.mult)
+            nc.vector.tensor_tensor(pages[s % 3][:].indirect(put[:]), h_tiles[s][:], wgs_sb[:], ALU.mult)
 
         def read(s):
-            b, t = divmod(s, PACK)
-            nc.vector.tensor_tensor(x_sb[b][:, t, :], pages[s % 2][:].indirect(fetch[:]), wgt_sb[:], ALU.mult)
+            nc.vector.tensor_tensor(x_rows[s], pages[s % 3][:].indirect(fetch[:]), wgt_sb[:], ALU.mult)
 
-        def add_sand(b, ms):
-            rows = lambda tile: tile[:, :, ms].rearrange("p t (c i) -> p c t i", i=4)
-            nc.vector.tensor_tensor(
-                z_bf[:, ms, :].rearrange("p (c i) t -> p c t i", i=4), rows(x_sb[b]), rows(sand_sb[b]), ALU.add)
+        def add_last_sand(mh):
+            ms = slice(half * mh, half * (mh + 1))
+            rows = [tile[:, :, ms].rearrange("p e (c i) -> p c e i", i=4) for tile in (x_two[-1], sand_sb[1][:, 2:4])]
+            words = z_two[mh][:, 1, :].bitcast(BF16)
+            nc.vector.tensor_tensor(words.rearrange("p (c i e) -> p c e i", i=4, e=2), rows[0], rows[1], ALU.add)
 
-        def quantize_z(b, ms):
-            nc.vector.quantize_mx(
-                z_w[b][:, ms].bitcast(FP8X4), z_s[b][:, ms], z_bf[:, ms, :].rearrange("p m t -> p (m t)"))
+        def z_words(b, mh):
+            return z_flat[b][mh].rearrange("p (m u) -> p m u", u=2)
+
+        def quantize_z(b, mh):
+            ms = slice(half * mh, half * (mh + 1))
+            nc.vector.quantize_mx(z_w[b][:, ms].bitcast(FP8X4), z_s[b][:, ms], z_flat[b][mh].bitcast(BF16))
 
         def round_w4(b):
             nc.scalar.copy(
@@ -238,76 +248,86 @@ def tile_list_nest_success_scores_kernel(
             flat = w4_bf[:].rearrange("p b n j -> p (b n j)")
             nc.vector.quantize_mx(w4_w[:, lo:hi].bitcast(FP8X4), w4_s[:, lo:hi], flat[:, PACK * lo : PACK * hi])
 
-        half = PM // 2
-        sums = {}
-        pairs = [held("pairs%d" % u, [P, CHUNKS, P, 2], BF16) for u in range(2)]
+        slices = HALVES * PACK
+        pairs = [held("pairs%d" % u, [P, CHUNKS * P], F32) for u in range(2)]
 
-        def turn_and_add(t):
-            u, e = divmod(t, 2)
-            for c in range(CHUNKS):
-                if (u, c // 2) not in sums:
-                    sums[u, c // 2] = bank((2 + 2 * u + c // 2) % 4)
-                block = sums[u, c // 2][:, P * (2 * (c % 2) + e) : P * (2 * (c % 2) + e + 1)]
-                ms = slice(P * c, P * (c + 1))
-                nc.tensor.matmul(block, lhsT=sand_sb[0][:, t, ms], rhs=ident[:], is_transpose=True, start=True, stop=False)
-                nc.tensor.matmul(block, lhsT=x_sb[0][:, t, ms], rhs=ident[:], is_transpose=True, start=False, stop=True)
-            if e == 1:
-                for mh in range(2):
-                    nc.scalar.copy(
-                        pairs[u][:, 2 * mh : 2 * mh + 2],
-                        sums[u, mh][:].rearrange("m (c e p) -> m c p e", c=2, e=2))
-
-        def turn_back():
+        def turn_and_add(b, u, first_bank):
+            sums = [bank(first_bank + mh) for mh in range(2)]
+            for e in range(2):
+                t = 2 * u + e
+                for c in range(CHUNKS):
+                    block = sums[c // 2][:, P * (2 * (c % 2) + e) : P * (2 * (c % 2) + e + 1)]
+                    ms = slice(P * c, P * (c + 1))
+                    turn(block, sand_sb[b][:, t, ms], True, False)
+                    turn(block, x_rows[PACK * b + t][:, ms], False, True)
             for mh in range(2):
-                back = bank(4 + mh)
-                for u in range(2):
-                    for c in range(2):
-                        words = pairs[u][:, 2 * mh + c].rearrange("m p e -> m (p e)").bitcast(F32)
-                        nc.tensor.transpose(back[:, half * u + P * c : half * u + P * (c + 1)], words, ident[:])
-                z_words = z_bf[:, half * mh : half * (mh + 1), :].rearrange("p m t -> p (m t)").bitcast(F32)
-                nc.scalar.copy(z_words.rearrange("p (m u) -> p m u", u=2), back[:].rearrange("p (u m) -> p m u", u=2))
+                nc.scalar.copy(
+                    pairs[u][:, half * mh : half * (mh + 1)].bitcast(BF16).rearrange("m (c p e) -> m c p e", c=2, e=2),
+                    sums[mh][:].rearrange("m (c e p) -> m c p e", c=2, e=2))
+
+        def turn_back(dst, u, mh):
+            for c in range(2):
+                cols = slice(P * (2 * mh + c), P * (2 * mh + c + 1))
+                turn(dst[:, P * c : P * (c + 1)], pairs[u][:, cols], True, True)
 
         opening = [(bank(2 * jc), bank(2 * jc + 1)) for jc in range(CHUNKS)]
         for jc in range(CHUNKS):
-            multiply23(opening[jc], 0, jc, 0)
+            multiply3(opening[jc][1], 0, jc, 0)
         for jc in range(CHUNKS):
-            multiply23(opening[jc], 0, jc, 1)
+            multiply2(opening[jc][0], 0, jc, 0)
+        for jc in range(CHUNKS):
+            multiply2(opening[jc][0], 0, jc, 1)
+            multiply3(opening[jc][1], 0, jc, 1)
             stronger23(opening[jc], 0, jc)
         round_w1(nc.scalar.copy, 0, 0, 0)
-        quantize_w1(0, 0, slice(0, 2))
+        round_w1(nc.vector.tensor_copy, 0, 0, 1)
+        quantize_w1(0, 0, slice(0, 4))
         round_w1(nc.vector.tensor_copy, 0, 1, 0)
+        round_w1(nc.scalar.copy, 0, 1, 1)
         quantize_w1(0, 1, slice(0, 2))
         strongest(0)
+        quantize_w1(0, 1, slice(2, 4))
         for jc in range(CHUNKS):
             evidence23(1, jc)
         strongest(1)
-        slices = HALVES * PACK
+        enter(0)
         for s in range(slices):
-            enter(s)
-            if s == 0:
-                for a in range(PASSES):
-                    round_w1(nc.scalar.copy, 0, a, 1)
-                    quantize_w1(0, a, slice(2, 4))
             if s == 2:
                 for a in range(PASSES):
                     quantize_w1(1, a, slice(0, 4))
-            if s == 4:
-                for b in range(HALVES):
-                    round_w4(b)
             if s + 2 < slices:
                 strongest(s + 2)
+            if s + 1 < slices:
+                enter(s + 1)
             if s == 1:
                 for a in range(PASSES):
                     for u in range(2):
                         round_w1(nc.scalar.copy, 1, a, u)
+            if s == 2:
+                for b in range(HALVES):
+                    round_w4(b)
+                quantize_w4(0, 512)
+                quantize_w4(512, 768)
+            if s == slices - 2:
+                turn_and_add(0, 0, 2)
+                turn_and_add(0, 1, 0)
+                for mh in range(2):
+                    back = bank(4 + mh)
+                    for u in range(2):
+                        turn_back(back[:, half * u : half * (u + 1)], u, mh)
+                    nc.scalar.copy(z_words(0, mh), back[:].rearrange("p (u m) -> p m u", u=2))
+                for mh in range(2):
+                    quantize_z(0, mh)
+                turn_and_add(1, 0, 2)
+                back = bank(0)
+                for mh in range(2):
+                    turn_back(back[:, half * mh : half * (mh + 1)], 0, mh)
+                for mh in range(2):
+                    nc.scalar.copy(z_two[mh][:, 0, :], back[:, half * mh : half * (mh + 1)])
             read(s)
-        for t in range(PACK):
-            turn_and_add(t)
-        turn_back()
-        quantize_z(0, slice(0, PM))
 
         res = held("res", [P, OUT_TILES, PM], F32)
-        y = {(mh, c): bank((6 + OUT_TILES * mh + c) % 8) for mh in range(2) for c in range(OUT_TILES)}
+        y = {(mh, c): bank((4, 5, 6, 7, 1, 2)[OUT_TILES * mh + c]) for mh in range(2) for c in range(OUT_TILES)}
 
         def score(b, mh, c):
             ms = slice(half * mh, half * (mh + 1))
@@ -317,16 +337,14 @@ def tile_list_nest_success_scores_kernel(
                 rhs=z_w[b][:, ms].bitcast(FP8X4), rhs_scale=z_s[b][:, ms],
                 start=(b == 0), stop=(b == HALVES - 1))
 
-        quantize_w4(0, 512)
-        add_sand(1, slice(0, half))
-        quantize_w4(512, 768)
         for mh, c in y:
             score(0, mh, c)
+        for mh, copy in enumerate((nc.scalar.copy, nc.vector.tensor_copy)):
+            add_last_sand(mh)
+            copy(z_words(1, mh), z_two[mh][:].rearrange("p u m -> p m u"))
         for mh in range(2):
             ms = slice(half * mh, half * (mh + 1))
-            if mh == 1:
-                add_sand(1, ms)
-            quantize_z(1, ms)
+            quantize_z(1, mh)
             for c in range(OUT_TILES):
                 score(1, mh, c)
                 nc.scalar.activation(res[:, c, ms], y[mh, c][:, 0:half], ACT.Tanh, bias=b4_sb[:, c : c + 1])

from contextlib import ExitStack

import concourse.mybir as mybir
from concourse.masks import make_identity

K, H, N, T, S, T2, PM = 1024, 1024, 384, 2048, 512, 1024, 512
FLOPS = 2 * (3 * K * H * S + H * N * PM)

F32 = mybir.dt.float32
BF16 = mybir.dt.bfloat16
I32 = mybir.dt.int32
U32 = mybir.dt.uint32
U16 = mybir.dt.uint16
U8 = mybir.dt.uint8
FP8X4 = mybir.dt.float8_e4m3fn_x4
FP4X4 = mybir.dt.float4_e2m1fn_x4
ALU = mybir.AluOpType
ACT = mybir.ActivationFunctionType

P = 128
PACK = 4
KP = P * PACK
PASSES = K // KP
HALVES = H // KP
CHUNKS = S // P
OUT_TILES = N // P


def tile_list_nest_success_scores_kernel(
    tc, tab_words, tab_scales, offs, offs2, offs3, w1, b1, w2_words, w2_scales,
    w3_words, w3_scales, wgs, wgt, sand, w4, b4, out,
):
    nc = tc.nc
    with ExitStack() as ctx:
        lists = ctx.enter_context(tc.tile_pool(name="lists", bufs=1))
        keep = ctx.enter_context(tc.tile_pool(name="keep", bufs=1))
        ring = ctx.enter_context(tc.tile_pool(name="ring", bufs=2))
        ring3 = ctx.enter_context(tc.tile_pool(name="ring3", bufs=3))
        psum = ctx.enter_context(tc.psum_pool(name="psum", bufs=1))

        def held(name, shape, dtype):
            return keep.tile(shape, dtype, name=name, align_bytes=64)

        pick = lists.tile([P, S // 16], U16, name="pick")
        put = lists.tile([P, S // 16], U16, name="put")
        fetch = lists.tile([P, PM // 16], U16, name="fetch")

        tab_s = held("tab_s", [P, PASSES * T], U8)
        w23_s = held("w23_s", [P, PASSES * H], U8)
        pages = [held("page%d" % i, [P, T2], F32) for i in range(3)]
        ident = held("ident", [P, P], F32)
        nc.vector.memset(tab_s[:].bitcast(I32), 0)
        for page in pages:
            nc.vector.memset(page[:], 0.0)

        tab_w = [held("tab_w%d" % a, [P, T], I32) for a in range(PASSES)]
        w2_w = [held("w2_w%d" % b, [P, PASSES, KP], I32) for b in range(HALVES)]
        w3_w = [held("w3_w%d" % b, [P, PASSES, 2 * KP], U8) for b in range(HALVES)]
        w1_raw = {(b, a): held("w1_raw%d%d" % (b, a), [P, PACK, KP], F32) for b in range(HALVES) for a in range(PASSES)}
        sand_sb = [held("sand%d" % b, [P, PACK, PM], F32) for b in range(HALVES)]
        w4_raw = held("w4_raw", [P, HALVES, PACK, N], F32)
        wgs_sb = held("wgs_sb", [P, S], F32)
        wgt_sb = held("wgt_sb", [P, PM], F32)
        b1_sb = held("b1_sb", [P, HALVES, PACK], F32)
        b4_sb = held("b4_sb", [P, OUT_TILES], F32)

        def load_scales(queue, plane, first_row, scales, quadrants):
            for q in quadrants:
                rows = plane[32 * q + first_row : 32 * q + first_row + 4, :].bitcast(I32)
                queue.dma_start(
                    rows.rearrange("r (a c) -> r a c", a=PASSES),
                    scales[:, 4 * q : 4 * q + 4, :].bitcast(I32).rearrange("a r c -> r a c"),
                )

        def load_w23(b):
            cols = slice(KP * b, KP * (b + 1))
            nc.sync.dma_start(w2_w[b][:], w2_words[:, :, cols, :].rearrange("a p c i -> p a (c i)").bitcast(I32))
            nc.sync.dma_start(
                w3_w[b][:].bitcast(I32),
                w3_words[:, :, 2 * KP * b : 2 * KP * (b + 1)].bitcast(I32).rearrange("a p c -> p a c"),
            )

        def load_w1(b):
            for a in range(PASSES):
                rows = w1[KP * a : KP * (a + 1), KP * b : KP * (b + 1)]
                nc.sync.dma_start(w1_raw[b, a][:], rows.rearrange("(p j) c -> p j c", j=PACK))

        def load_tab(a):
            nc.sync.dma_start(tab_w[a][:], tab_words[a].rearrange("p t i -> p (t i)").bitcast(I32))

        def load_sand(b):
            nc.sync.dma_start(sand_sb[b][:], sand[KP * b : KP * (b + 1), :].rearrange("(p j) m -> p j m", j=PACK))

        nc.sync.dma_start(pick[:], offs)
        load_scales(nc.sync, w23_s, 0, w3_scales, range(4))
        load_scales(nc.sync, w23_s, 4, w2_scales, range(2))
        load_tab(0)
        load_scales(nc.sync, tab_s, 0, tab_scales, range(4))
        load_w23(0)
        load_tab(1)
        load_scales(nc.sync, w23_s, 4, w2_scales, range(2, 4))
        load_w23(1)
        load_w1(0)
        nc.gpsimd.dma_start(b1_sb[:], b1.rearrange("(b p t) -> p b t", b=HALVES, t=PACK))
        make_identity(nc, ident[:])
        nc.sync.dma_start(put[:], offs2)
        nc.sync.dma_start(wgs_sb[:], wgs)
        nc.sync.dma_start(fetch[:], offs3)
        nc.sync.dma_start(wgt_sb[:], wgt)
        load_w1(1)
        load_sand(0)
        nc.sync.dma_start(w4_raw[:], w4.rearrange("(b p j) n -> p b j n", b=HALVES, j=PACK))
        load_sand(1)
        with nc.allow_non_contiguous_dma(reason="one bias value a partition"):
            nc.sync.dma_start(b4_sb[:], b4.rearrange("(c p) -> p c", p=P))

        v_w = [held("v_w%d" % a, [P, S], U32) for a in range(PASSES)]
        v_s = [held("v_s%d" % a, [P, S], U8) for a in range(PASSES)]
        for a in range(PASSES):
            nc.vector.tensor_copy(v_s[a][:], tab_s[:, T * a : T * (a + 1)].indirect(pick[:]))
            nc.vector.tensor_copy(v_w[a][:], tab_w[a][:].bitcast(U32).indirect(pick[:]))

        m_t = {(b, jc): held("m_t%d%d" % (b, jc), [P, 2, P, 2], F32) for b in range(HALVES) for jc in range(CHUNKS)}

        def bank(i):
            return psum.tile([P, KP], F32, name="bank%d" % i)

        def multiply(acc, words, plane, b, jc, a):
            js = slice(P * jc, P * (jc + 1))
            nc.tensor.matmul_mx(
                acc[:], lhsT=v_w[a][:, js].bitcast(FP8X4), lhsT_scale=v_s[a][:, js],
                rhs=words, rhs_scale=plane[:, H * a + KP * b : H * a + KP * (b + 1)],
                start=(a == 0), stop=(a == PASSES - 1))

        def multiply2(acc, b, jc, a):
            multiply(acc, w2_w[b][:, a, :].bitcast(FP8X4), w23_s[4:P, :], b, jc, a)

        def multiply3(acc, b, jc, a):
            multiply(acc, w3_w[b][:, a, :].bitcast(FP4X4), w23_s[:, :], b, jc, a)

        def stronger23(banks, b, jc):
            size = ring.tile([P, 2, P, 2], F32, name="size")
            dealt = [acc[:].rearrange("p (q u e) -> p u q e", u=2, e=2) for acc in banks]
            nc.scalar.activation(size[:], dealt[0], ACT.Abs)
            nc.vector.tensor_tensor(m_t[b, jc][:], dealt[1], size[:], ALU.max)

        def evidence23(b, jc):
            banks = (bank(4 + 2 * (jc % 2)), bank(5 + 2 * (jc % 2)))
            for a in range(PASSES):
                multiply2(banks[0], b, jc, a)
                multiply3(banks[1], b, jc, a)
            stronger23(banks, b, jc)

        w1_bf = {key: held("w1_bf%d%d" % key, [P, PACK, P, PACK], BF16) for key in w1_raw}
        w1_w = {key: held("w1_w%d%d" % key, [P, KP], U32) for key in w1_raw}
        w1_s = {key: held("w1_s%d%d" % key, [P, KP], U8) for key in w1_raw}

        def round_w1(copy, b, a, u):
            src = w1_raw[b, a][:].rearrange("p j (m u e) -> p u m j e", u=2, e=2)[:, u]
            dst = w1_bf[b, a][:, 2 * u : 2 * u + 2].rearrange("p e m j -> p m j e")
            copy(dst, src)

        def quantize_w1(b, a, ts):
            cols = slice(P * ts.start, P * ts.stop)
            nc.vector.quantize_mx(
                w1_w[b, a][:, cols].bitcast(FP8X4), w1_s[b, a][:, cols],
                w1_bf[b, a][:, ts].rearrange("p t m j -> p (t m j)"))

        h_tiles = {}

        def turn(dst, src, start, stop):
            nc.tensor.matmul(dst, lhsT=src, rhs=ident[:], is_transpose=True, start=start, stop=stop)

        def strongest(s):
            b, t = divmod(s, PACK)
            blocks = [slice(P * jc, P * (jc + 1)) for jc in range(CHUNKS)]
            m_rows = [m_t[b, jc][:, t // 2, :, t % 2] for jc in range(CHUNKS)]
            turned = bank(2 * (s % 2))
            for jc in range(CHUNKS):
                turn(turned[:, blocks[jc]], m_rows[jc], True, True)
            e1 = bank(2 * (s % 2) + 1)
            cols = slice(P * t, P * (t + 1))
            for a in range(PASSES):
                nc.tensor.matmul_mx(
                    e1[:], lhsT=w1_w[b, a][:, cols].bitcast(FP8X4), lhsT_scale=w1_s[b, a][:, cols],
                    rhs=v_w[a][:].bitcast(FP8X4), rhs_scale=v_s[a][:],
                    start=(a == 0), stop=(a == PASSES - 1))
            m23 = ring.tile([P, S], F32, name="m23")
            h = ring3.tile([P, S], F32, name="h")
            bias = b1_sb[:, b, t : t + 1]
            h_tiles[s] = h
            if s < 2:
                nc.scalar.copy(m23[:], turned[:])
                nc.vector.scalar_tensor_tensor(h[:], e1[:], bias, m23[:], ALU.add, ALU.max)
                return
            nc.scalar.activation(m23[:], turned[:], ACT.Copy, scale=-1.0)
            first = ring.tile([P, S], F32, name="first")
            nc.scalar.activation(first[:], e1[:], ACT.Identity, bias=bias)
            lead = bank(2 * (s % 2))
            for jc in range(CHUNKS):
                turn(lead[:, blocks[jc]], m23[:, blocks[jc]], True, False)
                turn(lead[:, blocks[jc]], first[:, blocks[jc]], False, True)
            excess = x_rows[s - 2]
            nc.scalar.activation(excess, lead[:], ACT.Relu)
            total = bank(2 * (s % 2) + 1)
            for jc in range(CHUNKS):
                turn(total[:, blocks[jc]], m_rows[jc], True, False)
                turn(total[:, blocks[jc]], excess[:, blocks[jc]], False, True)
            nc.scalar.copy(h[:], total[:])

        half = PM // 2
        x_two = [held("x%d" % i, [P, 2, PM], F32) for i in range(2 * HALVES)]
        x_rows = [x_two[s // 2][:, s % 2, :] for s in range(HALVES * PACK)]
        z_last = [held("z_last%d" % mh, [P, PM], F32) for mh in range(2)]
        z_flat = [x_rows[-2:], [tile[:] for tile in z_last]]
        z_two = [held("z_two%d" % mh, [P, 2, half], F32) for mh in range(2)]
        z_w = [held("z_w%d" % b, [P, PM], U32) for b in range(HALVES)]
        z_s = [held("z_s%d" % b, [P, PM], U8) for b in range(HALVES)]
        w4_bf = held("w4_bf", [P, HALVES, N, PACK], BF16)
        w4_w = held("w4_w", [P, HALVES * N], U32)
        w4_s = held("w4_s", [P, HALVES * N], U8)

        def enter(s):
            nc.vector.tensor_tensor(pages[s % 3][:].indirect(put[:]), h_tiles[s][:], wgs_sb[:], ALU.mult)

        def read(s):
            nc.vector.tensor_tensor(x_rows[s], pages[s % 3][:].indirect(fetch[:]), wgt_sb[:], ALU.mult)

        def add_last_sand(mh):
            ms = slice(half * mh, half * (mh + 1))
            rows = [tile[:, :, ms].rearrange("p e (c i) -> p c e i", i=4) for tile in (x_two[-1], sand_sb[1][:, 2:4])]
            words = z_two[mh][:, 1, :].bitcast(BF16)
            nc.vector.tensor_tensor(words.rearrange("p (c i e) -> p c e i", i=4, e=2), rows[0], rows[1], ALU.add)

        def z_words(b, mh):
            return z_flat[b][mh].rearrange("p (m u) -> p m u", u=2)

        def quantize_z(b, mh):
            ms = slice(half * mh, half * (mh + 1))
            nc.vector.quantize_mx(z_w[b][:, ms].bitcast(FP8X4), z_s[b][:, ms], z_flat[b][mh].bitcast(BF16))

        def round_w4(b):
            nc.scalar.copy(
                w4_bf[:, b].rearrange("p (c i) j -> p c j i", i=4),
                w4_raw[:, b].rearrange("p j (c i) -> p c j i", i=4))

        def quantize_w4(lo, hi):
            flat = w4_bf[:].rearrange("p b n j -> p (b n j)")
            nc.vector.quantize_mx(w4_w[:, lo:hi].bitcast(FP8X4), w4_s[:, lo:hi], flat[:, PACK * lo : PACK * hi])

        slices = HALVES * PACK
        pairs = [held("pairs%d" % u, [P, CHUNKS * P], F32) for u in range(2)]

        def turn_and_add(b, u, first_bank):
            sums = [bank(first_bank + mh) for mh in range(2)]
            for e in range(2):
                t = 2 * u + e
                for c in range(CHUNKS):
                    block = sums[c // 2][:, P * (2 * (c % 2) + e) : P * (2 * (c % 2) + e + 1)]
                    ms = slice(P * c, P * (c + 1))
                    turn(block, sand_sb[b][:, t, ms], True, False)
                    turn(block, x_rows[PACK * b + t][:, ms], False, True)
            for mh in range(2):
                nc.scalar.copy(
                    pairs[u][:, half * mh : half * (mh + 1)].bitcast(BF16).rearrange("m (c p e) -> m c p e", c=2, e=2),
                    sums[mh][:].rearrange("m (c e p) -> m c p e", c=2, e=2))

        def turn_back(dst, u, mh):
            for c in range(2):
                cols = slice(P * (2 * mh + c), P * (2 * mh + c + 1))
                turn(dst[:, P * c : P * (c + 1)], pairs[u][:, cols], True, True)

        opening = [(bank(2 * jc), bank(2 * jc + 1)) for jc in range(CHUNKS)]
        for jc in range(CHUNKS):
            multiply3(opening[jc][1], 0, jc, 0)
        for jc in range(CHUNKS):
            multiply2(opening[jc][0], 0, jc, 0)
        for jc in range(CHUNKS):
            multiply2(opening[jc][0], 0, jc, 1)
            multiply3(opening[jc][1], 0, jc, 1)
            stronger23(opening[jc], 0, jc)
        round_w1(nc.scalar.copy, 0, 0, 0)
        round_w1(nc.vector.tensor_copy, 0, 0, 1)
        quantize_w1(0, 0, slice(0, 4))
        round_w1(nc.vector.tensor_copy, 0, 1, 0)
        round_w1(nc.scalar.copy, 0, 1, 1)
        quantize_w1(0, 1, slice(0, 2))
        strongest(0)
        quantize_w1(0, 1, slice(2, 4))
        for jc in range(CHUNKS):
            evidence23(1, jc)
        strongest(1)
        enter(0)
        for s in range(slices):
            if s == 2:
                for a in range(PASSES):
                    quantize_w1(1, a, slice(0, 4))
            if s + 2 < slices:
                strongest(s + 2)
            if s + 1 < slices:
                enter(s + 1)
            if s == 1:
                for a in range(PASSES):
                    for u in range(2):
                        round_w1(nc.scalar.copy, 1, a, u)
            if s == 2:
                for b in range(HALVES):
                    round_w4(b)
                quantize_w4(0, 512)
                quantize_w4(512, 768)
            if s == slices - 2:
                turn_and_add(0, 0, 2)
                turn_and_add(0, 1, 0)
                for mh in range(2):
                    back = bank(4 + mh)
                    for u in range(2):
                        turn_back(back[:, half * u : half * (u + 1)], u, mh)
                    nc.scalar.copy(z_words(0, mh), back[:].rearrange("p (u m) -> p m u", u=2))
                for mh in range(2):
                    quantize_z(0, mh)
                turn_and_add(1, 0, 2)
                back = bank(0)
                for mh in range(2):
                    turn_back(back[:, half * mh : half * (mh + 1)], 0, mh)
                for mh in range(2):
                    nc.scalar.copy(z_two[mh][:, 0, :], back[:, half * mh : half * (mh + 1)])
            read(s)

        res = held("res", [P, OUT_TILES, PM], F32)
        y = {(mh, c): bank((4, 5, 6, 7, 1, 2)[OUT_TILES * mh + c]) for mh in range(2) for c in range(OUT_TILES)}

        def score(b, mh, c):
            ms = slice(half * mh, half * (mh + 1))
            cols = slice(N * b + P * c, N * b + P * (c + 1))
            nc.tensor.matmul_mx(
                y[mh, c][:, 0:half], lhsT=w4_w[:, cols].bitcast(FP8X4), lhsT_scale=w4_s[:, cols],
                rhs=z_w[b][:, ms].bitcast(FP8X4), rhs_scale=z_s[b][:, ms],
                start=(b == 0), stop=(b == HALVES - 1))

        for mh, c in y:
            score(0, mh, c)
        for mh, copy in enumerate((nc.scalar.copy, nc.vector.tensor_copy)):
            add_last_sand(mh)
            copy(z_words(1, mh), z_two[mh][:].rearrange("p u m -> p m u"))
        for mh in range(2):
            ms = slice(half * mh, half * (mh + 1))
            quantize_z(1, mh)
            for c in range(OUT_TILES):
                score(1, mh, c)
                nc.scalar.activation(res[:, c, ms], y[mh, c][:, 0:half], ACT.Tanh, bias=b4_sb[:, c : c + 1])
                nc.sync.dma_start(out[P * c : P * (c + 1), ms], res[:, c, ms])
